import numpy as np
import ml_dtypes


def mxq(x, axis, fmt="e4m3"):
    dtype, down = {"e4m3": (ml_dtypes.float8_e4m3fn, 7), "e5m2": (ml_dtypes.float8_e5m2, 14)}[fmt]
    v = np.moveaxis(np.asarray(x, np.float32).astype(ml_dtypes.bfloat16).astype(np.float64), axis, -1)
    blocks = v.reshape(v.shape[:-1] + (-1, 32))
    amax = np.abs(blocks).max(-1, keepdims=True)
    byte = np.maximum(np.where(amax > 0, np.frexp(amax)[1] - 1 + 127, 0) - down, 1)
    scale = np.exp2(byte - 127.0)
    codes = (blocks / scale).astype(np.float32).astype(dtype).astype(np.float64)
    return np.moveaxis((codes * scale).reshape(v.shape), -1, axis)


WIDE = False


def mx_kscale(k):
    if not WIDE:
        return np.ones(k)
    levels = np.array([10, -10, 5, -5, 0])
    if k % 512:
        return np.exp2(np.random.permutation(np.resize(levels, k // 32))).repeat(32)
    a = np.empty((k // 512, 16))
    for p in range(k // 512):
        a[p, :8] = np.random.permutation(np.resize(levels, 8))
        for g in range(8):
            far = levels[np.abs(levels - a[p, g]) >= 10]
            a[p, g + 8] = far[np.random.randint(len(far))]
    return np.exp2(a.ravel()).repeat(32)


def f64(x):
    return np.asarray(x).astype(np.float64)


def striped(idx):
    return np.tile(idx.reshape(-1, 16).T, (8, 1)).astype(np.uint16)


def unstriped(offs):
    return offs[:16].T.reshape(-1).astype(np.int64)


E2M1 = np.array([0.0, 0.5, 1.0, 1.5, 2.0, 3.0, 4.0, 6.0, -0.0, -0.5, -1.0, -1.5, -2.0, -3.0, -4.0, -6.0])


def pack_fp4(w):
    k, n = w.shape
    w = f64(np.asarray(w, np.float32).astype(ml_dtypes.bfloat16)).reshape(k // 32, 32, n)
    amax = np.abs(w).max(1)
    mant, ex = np.frexp(amax / 6.0)
    byte = np.clip(np.where(amax > 0, np.where(mant > 0.5, ex, ex - 1) + 127, 1), 1, 254)
    scaled = (w * np.exp2(127.0 - byte)[:, None, :]).reshape(k, n).astype(np.float32)
    c = np.ascontiguousarray(scaled.reshape(k // 512, 128, 4, n).transpose(0, 1, 3, 2)).astype(ml_dtypes.float4_e2m1fn).view(np.uint8) & 0xF
    words = (c[..., 0::2] | (c[..., 1::2] << 4)).reshape(k // 512, 128, 2 * n)
    return np.ascontiguousarray(words), np.ascontiguousarray(byte.astype(np.uint8).reshape(k // 512, 16, n))


def unpack_fp4(words, scales):
    g, _, n = scales.shape
    words = np.ascontiguousarray(words).reshape(g, 128, n, 2)
    nib = np.empty((g, 128, n, 4), np.uint8)
    nib[..., 0::2] = words & 0xF
    nib[..., 1::2] = words >> 4
    vals = E2M1[nib] * np.repeat(np.exp2(scales.astype(np.float64) - 127.0), 8, axis=1)[..., None]
    return vals.transpose(0, 1, 3, 2).reshape(g * 512, n)


def relu(v):
    return np.maximum(v, 0.0)


K, T, S, H, N = 1024, 2048, 512, 512, 128


def setup_inputs():
    n = np.random.standard_normal
    s = mx_kscale(K)[:, None]
    u = mx_kscale(H)
    packed_w2 = pack_fp4(n((H, N)) / np.sqrt(H) / u[:, None])
    return {
        "xT": (n((K, T)) * s).astype(np.float32),
        "w1": (n((K, H)) / np.sqrt(K) / s).astype(np.float32),
        "w2_words": packed_w2[0],
        "w2_scales": packed_w2[1],
        "gamma": (np.random.uniform(0.5, 1.5, (H, 1)) * u[:, None]).astype(np.float32),
        "offs": striped(np.random.permutation(T)[:S]),
    }


def reference(xT, w1, w2_words, w2_scales, gamma, offs):
    xq = mxq(f64(xT)[:, unstriped(offs)], 0, "e4m3")
    h = mxq(f64(w1), 0, "e4m3").T @ xq
    hn = (h - h.mean(axis=1, keepdims=True)) / np.sqrt(h.var(axis=1, keepdims=True) + 1e-5)
    z = relu(f64(gamma) * hn)
    return unpack_fp4(w2_words, w2_scales).T @ mxq(z, 0, "e4m3")

@@ -1,0 +1,210 @@
+from contextlib import ExitStack
+
+import concourse.mybir as mybir
+
+K, T, S, H, N = 1024, 2048, 512, 512, 128
+FLOPS = 2 * K * H * S + 2 * H * N * S
+
+F32 = mybir.dt.float32
+BF16 = mybir.dt.bfloat16
+U32 = mybir.dt.uint32
+I32 = mybir.dt.int32
+U16 = mybir.dt.uint16
+U8 = mybir.dt.uint8
+FP8X4 = mybir.dt.float8_e4m3fn_x4
+FP4X4 = mybir.dt.float4_e2m1fn_x4
+ACT = mybir.ActivationFunctionType
+ALU = mybir.AluOpType
+
+P = 128
+PACK = 4
+K_PASS = P * PACK
+PASSES = K // K_PASS
+EPS = 1e-5
+CHUNK = 128
+CHUNKS = S // CHUNK
+
+
+def tile_picked_inorm_relu_e_kernel(tc, xT, w1, w2_words, w2_scales, gamma, offs, out):
+    nc = tc.nc
+    with ExitStack() as ctx:
+        sb = ctx.enter_context(tc.tile_pool(name="sb", bufs=1))
+        ps = ctx.enter_context(tc.psum_pool(name="ps", bufs=1))
+
+        offsets = sb.tile([P, S // 16], U16, name="offsets")
+        x_raw = [[sb.tile([P, T], F32, name=f"x_raw{g}{j}") for j in range(PACK)] for g in range(PASSES)]
+        w_raw = [[sb.tile([P, 2, H], F32, name=f"w_raw{g}{u}") for u in range(2)] for g in range(PASSES)]
+        x_bf = [sb.tile([P, S, PACK], BF16, name=f"x_bf{g}", align_bytes=64) for g in range(PASSES)]
+        x_codes = [sb.tile([P, S], U32, name=f"x_codes{g}", align_bytes=64) for g in range(PASSES)]
+        x_scales = [sb.tile([P, S], U8, name=f"x_scales{g}", align_bytes=64) for g in range(PASSES)]
+        w_bf = [[sb.tile([P, 2, P, PACK], BF16, name=f"w_bf{g}{v}", align_bytes=64) for v in range(2)] for g in range(PASSES)]
+        w_codes = [[sb.tile([P, P], U32, name=f"w_codes{g}{t}", align_bytes=64) for t in range(PACK)] for g in range(PASSES)]
+        w_scales = [[sb.tile([P, P], U8, name=f"w_scales{g}{t}", align_bytes=64) for t in range(PACK)] for g in range(PASSES)]
+        w2_codes = sb.tile([P, 2 * N], U8, name="w2_codes", align_bytes=64)
+        w2_plane = sb.tile([P, N], U8, name="w2_plane", align_bytes=64)
+        gam = sb.tile([P, PACK], F32, name="gam")
+        h = [ps.tile([P, S], F32, name=f"h{t}") for t in range(PACK)]
+
+        def load_x(g, j):
+            rows = xT[g * K_PASS : (g + 1) * K_PASS, :].rearrange("(p j) t -> p j t", j=PACK)
+            nc.sync.dma_start(out=x_raw[g][j][:], in_=rows[:, j, :])
+
+        def load_w(g, u):
+            rows = w1[g * K_PASS : (g + 1) * K_PASS, :].rearrange("(p j) c -> p j c", j=PACK)
+            nc.sync.dma_start(out=w_raw[g][u][:], in_=rows[:, 2 * u : 2 * u + 2, :])
+
+        def gather_x(g, j, lo, hi):
+            nc.vector.tensor_copy(
+                out=x_bf[g][:, lo:hi, j],
+                in_=x_raw[g][j][:].indirect(offsets[:, lo // 16 : hi // 16]),
+            )
+
+        def quantize_x(g, lo, hi):
+            nc.vector.quantize_mx(
+                out=x_codes[g][:, lo:hi].bitcast(FP8X4),
+                scales=x_scales[g][:, lo:hi],
+                in_=x_bf[g][:, lo:hi, :].rearrange("p s j -> p (s j)"),
+            )
+
+        def deal_w(copy, g, u, v):
+            copy(
+                out=w_bf[g][v][:, :, :, 2 * u : 2 * u + 2].rearrange("p t m j -> p m t j"),
+                in_=w_raw[g][u][:].rearrange("p j (m t) -> p m t j", t=PACK)[:, :, 2 * v : 2 * v + 2, :],
+            )
+
+        def quantize_w(g, t):
+            nc.vector.quantize_mx(
+                out=w_codes[g][t][:].bitcast(FP8X4),
+                scales=w_scales[g][t][:],
+                in_=w_bf[g][t // 2][:, t % 2, :, :].rearrange("p m j -> p (m j)"),
+            )
+
+        def product1(g, t):
+            nc.tensor.matmul_mx(
+                out=h[t][:],
+                lhsT=w_codes[g][t][:].bitcast(FP8X4),
+                lhsT_scale=w_scales[g][t][:],
+                rhs=x_codes[g][:].bitcast(FP8X4),
+                rhs_scale=x_scales[g][:],
+                start=(g == 0),
+                stop=(g == PASSES - 1),
+            )
+
+        load_x(0, 0)
+        nc.sync.dma_start(offsets[:], offs)
+        for j in range(1, PACK):
+            load_x(0, j)
+        load_w(0, 0)
+        load_w(0, 1)
+        for j in range(PACK):
+            load_x(1, j)
+        load_w(1, 0)
+        load_w(1, 1)
+
+        nc.gpsimd.memset(w2_plane[:].bitcast(I32), 0)
+        nc.gpsimd.dma_start(out=gam[:], in_=gamma.rearrange("(p t) o -> p (t o)", t=PACK))
+        nc.gpsimd.dma_start(out=w2_codes[:].bitcast(I32), in_=w2_words[0].bitcast(I32))
+        for q in range(4):
+            nc.gpsimd.dma_start(
+                out=w2_plane[32 * q : 32 * q + 4, :].bitcast(I32),
+                in_=w2_scales[0, 4 * q : 4 * q + 4, :].bitcast(I32),
+            )
+        pre = [sb.tile([P, 2], F32, name=f"pre{t}") for t in range(PACK)]
+        for t in range(PACK):
+            nc.gpsimd.tensor_copy(out=pre[t][:, 0:1], in_=gam[:, t : t + 1])
+
+        warm_in = sb.tile([P, 1], F32, name="warm_in")
+        warm_out = sb.tile([P, 1], F32, name="warm_out")
+        nc.vector.memset(warm_in[:], 1.0)
+        nc.scalar.activation(out=warm_out[:], in_=warm_in[:], func=ACT.Abs_reciprocal_sqrt, bias=EPS)
+
+        for j in range(PACK):
+            gather_x(0, j, 0, S)
+        quantize_x(0, 0, S)
+        for u in range(2):
+            for v in range(2):
+                deal_w(nc.scalar.copy, 0, u, v)
+        gather_x(1, 0, 0, S)
+        for t in range(PACK):
+            quantize_w(0, t)
+            product1(0, t)
+
+        gather_x(1, 1, 0, S)
+        gather_x(1, 2, 0, S)
+        gather_x(1, 3, 0, S // 2)
+        gather_x(1, 3, S // 2, S)
+        quantize_x(1, 0, S // 2)
+        quantize_x(1, S // 2, S)
+        deal_w(nc.scalar.copy, 1, 0, 0)
+        deal_w(nc.scalar.copy, 1, 0, 1)
+        deal_w(nc.vector.tensor_copy, 1, 1, 0)
+        deal_w(nc.scalar.copy, 1, 1, 1)
+        for t in range(PACK):
+            quantize_w(1, t)
+            product1(1, t)
+
+        z_flat = [sb.tile([P, 2, S], BF16, name=f"z_flat{v}") for v in range(2)]
+        z_bf = sb.tile([P, S, PACK], BF16, name="z_bf", align_bytes=64)
+        post = []
+        for t in range(PACK):
+            stats = sb.tile([P, 2, 6], F32, name=f"stats{t}")
+            for half in range(2):
+                nc.vector.bn_stats(out=stats[:, half, :], in_=h[t][:, half * (S // 2) : (half + 1) * (S // 2)])
+            moments = sb.tile([P, 2], F32, name=f"moments{t}")
+            nc.vector.bn_aggr(out=moments[:], in_=stats[:].rearrange("p a b -> p (a b)"))
+            nc.gpsimd.tensor_scalar(
+                out=pre[t][:, 1:2], in0=moments[:, 0:1], scalar1=gam[:, t : t + 1], scalar2=-1.0, op0=ALU.mult, op1=ALU.mult
+            )
+            rstd = sb.tile([P, 1], F32, name=f"rstd{t}")
+            nc.scalar.activation(out=rstd[:], in_=moments[:, 1:2], func=ACT.Abs_reciprocal_sqrt, bias=EPS)
+            ab = sb.tile([P, 2], F32, name=f"ab{t}")
+            nc.scalar.activation(out=ab[:], in_=pre[t][:], func=ACT.Copy, scale=rstd[:])
+            post.append(ab)
+            if t < PACK - 1:
+                nc.scalar.activation(
+                    out=z_flat[t // 2][:, t % 2, :], in_=h[t][:], func=ACT.Relu, scale=ab[:, 0:1], bias=ab[:, 1:2]
+                )
+
+        nc.vector.tensor_copy(out=z_bf[:, :, 0:2], in_=z_flat[0][:].rearrange("p t s -> p s t"))
+        last = PACK - 1
+
+        def finish_z(c):
+            cols = slice(c * CHUNK, (c + 1) * CHUNK)
+            nc.scalar.activation(
+                out=z_flat[1][:, 1, cols], in_=h[last][:, cols], func=ACT.Relu, scale=post[last][:, 0:1], bias=post[last][:, 1:2]
+            )
+            nc.vector.tensor_copy(out=z_bf[:, cols, 2:4], in_=z_flat[1][:, :, cols].rearrange("p t s -> p s t"))
+
+        def product2(c):
+            cols = slice(c * CHUNK, (c + 1) * CHUNK)
+            z_codes = sb.tile([P, CHUNK], U32, name=f"z_codes{c}", align_bytes=64)
+            z_scales = sb.tile([P, CHUNK], U8, name=f"z_scales{c}", align_bytes=64)
+            nc.vector.quantize_mx(
+                out=z_codes[:].bitcast(FP8X4), scales=z_scales[:], in_=z_bf[:, cols, :].rearrange("p s j -> p (s j)")
+            )
+            acc = ps.tile([P, CHUNK], F32, name=f"acc{c}")
+            nc.tensor.matmul_mx(
+                out=acc[:],
+                lhsT=w2_codes[:].bitcast(FP4X4),
+                lhsT_scale=w2_plane[:],
+                rhs=z_codes[:].bitcast(FP8X4),
+                rhs_scale=z_scales[:],
+                start=True,
+                stop=True,
+            )
+            return acc
+
+        def store(c, acc):
+            cols = slice(c * CHUNK, (c + 1) * CHUNK)
+            result = sb.tile([P, CHUNK], F32, name=f"result{c}")
+            nc.scalar.copy(out=result[:], in_=acc[:])
+            nc.sync.dma_start(out=out[:, cols], in_=result[:])
+
+        accs = []
+        finish_z(0)
+        for c in range(CHUNKS):
+            if c + 1 < CHUNKS:
+                finish_z(c + 1)
+            accs.append(product2(c))
+        for c in range(CHUNKS):
+            store(c, accs[c])

@@ -32,8 +32,14 @@ def tile_picked_inorm_relu_e_kernel(tc, xT, w1, w2_words, w2_scales, gamma, offs
         ps = ctx.enter_context(tc.psum_pool(name="ps", bufs=1))
 
         offsets = sb.tile([P, S // 16], U16, name="offsets")
-        x_raw = [[sb.tile([P, T], F32, name=f"x_raw{g}{j}") for j in range(PACK)] for g in range(PASSES)]
-        w_raw = [[sb.tile([P, 2, H], F32, name=f"w_raw{g}{u}") for u in range(2)] for g in range(PASSES)]
+        x_pair = [sb.tile([P, 2, T], F32, name=f"x_pair{u}") for u in range(2)]
+        x_one = [sb.tile([P, T], F32, name=f"x_one{j}") for j in range(PACK)]
+        x_raw = [[x_pair[j // 2][:, j % 2, :] for j in range(PACK)], [x_one[j][:] for j in range(PACK)]]
+        w_whole = sb.tile([P, PACK, H], F32, name="w_whole")
+        w_half = [sb.tile([P, 2, H], F32, name=f"w_half{u}") for u in range(2)]
+        w_raw = [[w_whole[:, 2 * u : 2 * u + 2, :] for u in range(2)], [w_half[u][:] for u in range(2)]]
+        x_rows = [xT[g * K_PASS : (g + 1) * K_PASS, :].rearrange("(p j) t -> p j t", j=PACK) for g in range(PASSES)]
+        w_rows = [w1[g * K_PASS : (g + 1) * K_PASS, :].rearrange("(p j) c -> p j c", j=PACK) for g in range(PASSES)]
         x_bf = [sb.tile([P, S, PACK], BF16, name=f"x_bf{g}", align_bytes=64) for g in range(PASSES)]
         x_codes = [sb.tile([P, S], U32, name=f"x_codes{g}", align_bytes=64) for g in range(PASSES)]
         x_scales = [sb.tile([P, S], U8, name=f"x_scales{g}", align_bytes=64) for g in range(PASSES)]
@@ -45,18 +51,10 @@ def tile_picked_inorm_relu_e_kernel(tc, xT, w1, w2_words, w2_scales, gamma, offs
         gam = sb.tile([P, PACK], F32, name="gam")
         h = [ps.tile([P, S], F32, name=f"h{t}") for t in range(PACK)]
 
-        def load_x(g, j):
-            rows = xT[g * K_PASS : (g + 1) * K_PASS, :].rearrange("(p j) t -> p j t", j=PACK)
-            nc.sync.dma_start(out=x_raw[g][j][:], in_=rows[:, j, :])
-
-        def load_w(g, u):
-            rows = w1[g * K_PASS : (g + 1) * K_PASS, :].rearrange("(p j) c -> p j c", j=PACK)
-            nc.sync.dma_start(out=w_raw[g][u][:], in_=rows[:, 2 * u : 2 * u + 2, :])
-
         def gather_x(g, j, lo, hi):
             nc.vector.tensor_copy(
                 out=x_bf[g][:, lo:hi, j],
-                in_=x_raw[g][j][:].indirect(offsets[:, lo // 16 : hi // 16]),
+                in_=x_raw[g][j].indirect(offsets[:, lo // 16 : hi // 16]),
             )
 
         def quantize_x(g, lo, hi):
@@ -69,7 +67,7 @@ def tile_picked_inorm_relu_e_kernel(tc, xT, w1, w2_words, w2_scales, gamma, offs
         def deal_w(copy, g, u, v):
             copy(
                 out=w_bf[g][v][:, :, :, 2 * u : 2 * u + 2].rearrange("p t m j -> p m t j"),
-                in_=w_raw[g][u][:].rearrange("p j (m t) -> p m t j", t=PACK)[:, :, 2 * v : 2 * v + 2, :],
+                in_=w_raw[g][u].rearrange("p j (m t) -> p m t j", t=PACK)[:, :, 2 * v : 2 * v + 2, :],
             )
 
         def quantize_w(g, t):
@@ -90,16 +88,14 @@ def tile_picked_inorm_relu_e_kernel(tc, xT, w1, w2_words, w2_scales, gamma, offs
                 stop=(g == PASSES - 1),
             )
 
-        load_x(0, 0)
+        nc.sync.dma_start(out=x_pair[0][:], in_=x_rows[0][:, 0:2, :])
         nc.sync.dma_start(offsets[:], offs)
-        for j in range(1, PACK):
-            load_x(0, j)
-        load_w(0, 0)
-        load_w(0, 1)
+        nc.sync.dma_start(out=x_pair[1][:], in_=x_rows[0][:, 2:4, :])
+        nc.sync.dma_start(out=w_whole[:], in_=w_rows[0])
         for j in range(PACK):
-            load_x(1, j)
-        load_w(1, 0)
-        load_w(1, 1)
+            nc.sync.dma_start(out=x_one[j][:], in_=x_rows[1][:, j, :])
+        for u in range(2):
+            nc.sync.dma_start(out=w_half[u][:], in_=w_rows[1][:, 2 * u : 2 * u + 2, :])
 
         nc.gpsimd.memset(w2_plane[:].bitcast(I32), 0)
         nc.gpsimd.dma_start(out=gam[:], in_=gamma.rearrange("(p t) o -> p (t o)", t=PACK))
@@ -109,9 +105,16 @@ def tile_picked_inorm_relu_e_kernel(tc, xT, w1, w2_words, w2_scales, gamma, offs
                 out=w2_plane[32 * q : 32 * q + 4, :].bitcast(I32),
                 in_=w2_scales[0, 4 * q : 4 * q + 4, :].bitcast(I32),
             )
-        pre = [sb.tile([P, 2], F32, name=f"pre{t}") for t in range(PACK)]
+        neg_gam = sb.tile([P, PACK], F32, name="neg_gam")
+        nc.gpsimd.tensor_scalar(out=neg_gam[:], in0=gam[:], scalar1=-1.0, scalar2=0.0, op0=ALU.mult, op1=ALU.add)
+        moments = [sb.tile([P, 3], F32, name=f"moments{t}") for t in range(PACK)]
         for t in range(PACK):
-            nc.gpsimd.tensor_copy(out=pre[t][:, 0:1], in_=gam[:, t : t + 1])
+            nc.vector.memset(moments[t][:, 0:1], -1.0)
+        z_flat = [sb.tile([P, 2, S], BF16, name=f"z_flat{v}") for v in range(2)]
+        eps_first = sb.tile([P, 1], F32, name="eps_first")
+        eps = [eps_first[:]] + [z_flat[t // 2][:, t % 2, 0:2].bitcast(F32) for t in range(PACK - 1)]
+        for t in range(PACK):
+            nc.vector.tensor_scalar(out=eps[t], in0=moments[0][:, 0:1], scalar1=-EPS, scalar2=None, op0=ALU.mult)
 
         warm_in = sb.tile([P, 1], F32, name="warm_in")
         warm_out = sb.tile([P, 1], F32, name="warm_out")
@@ -143,26 +146,22 @@ def tile_picked_inorm_relu_e_kernel(tc, xT, w1, w2_words, w2_scales, gamma, offs
             quantize_w(1, t)
             product1(1, t)
 
-        z_flat = [sb.tile([P, 2, S], BF16, name=f"z_flat{v}") for v in range(2)]
         z_bf = sb.tile([P, S, PACK], BF16, name="z_bf", align_bytes=64)
         post = []
         for t in range(PACK):
             stats = sb.tile([P, 2, 6], F32, name=f"stats{t}")
             for half in range(2):
                 nc.vector.bn_stats(out=stats[:, half, :], in_=h[t][:, half * (S // 2) : (half + 1) * (S // 2)])
-            moments = sb.tile([P, 2], F32, name=f"moments{t}")
-            nc.vector.bn_aggr(out=moments[:], in_=stats[:].rearrange("p a b -> p (a b)"))
-            nc.gpsimd.tensor_scalar(
-                out=pre[t][:, 1:2], in0=moments[:, 0:1], scalar1=gam[:, t : t + 1], scalar2=-1.0, op0=ALU.mult, op1=ALU.mult
-            )
+            nc.vector.bn_aggr(out=moments[t][:, 1:3], in_=stats[:].rearrange("p a b -> p (a b)"))
             rstd = sb.tile([P, 1], F32, name=f"rstd{t}")
-            nc.scalar.activation(out=rstd[:], in_=moments[:, 1:2], func=ACT.Abs_reciprocal_sqrt, bias=EPS)
+            nc.scalar.activation(out=rstd[:], in_=moments[t][:, 2:3], func=ACT.Abs_reciprocal_sqrt, bias=eps[t])
             ab = sb.tile([P, 2], F32, name=f"ab{t}")
-            nc.scalar.activation(out=ab[:], in_=pre[t][:], func=ACT.Copy, scale=rstd[:])
+            nc.gpsimd.tensor_scalar(out=ab[:], in0=moments[t][:, 0:2], scalar1=rstd[:], scalar2=neg_gam[:, t : t + 1], op0=ALU.mult, op1=ALU.mult)
             post.append(ab)
-            if t < PACK - 1:
+            if t > 0:
+                s = t - 1
                 nc.scalar.activation(
-                    out=z_flat[t // 2][:, t % 2, :], in_=h[t][:], func=ACT.Relu, scale=ab[:, 0:1], bias=ab[:, 1:2]
+                    out=z_flat[s // 2][:, s % 2, :], in_=h[s][:], func=ACT.Relu, scale=post[s][:, 0:1], bias=post[s][:, 1:2]
                 )
 
         nc.vector.tensor_copy(out=z_bf[:, :, 0:2], in_=z_flat[0][:].rearrange("p t s -> p s t"))
@@ -173,7 +172,8 @@ def tile_picked_inorm_relu_e_kernel(tc, xT, w1, w2_words, w2_scales, gamma, offs
             nc.scalar.activation(
                 out=z_flat[1][:, 1, cols], in_=h[last][:, cols], func=ACT.Relu, scale=post[last][:, 0:1], bias=post[last][:, 1:2]
             )
-            nc.vector.tensor_copy(out=z_bf[:, cols, 2:4], in_=z_flat[1][:, :, cols].rearrange("p t s -> p s t"))
+            copy = nc.scalar.copy if c == CHUNKS - 1 else nc.vector.tensor_copy
+            copy(out=z_bf[:, cols, 2:4], in_=z_flat[1][:, :, cols].rearrange("p t s -> p s t"))
 
         def product2(c):
             cols = slice(c * CHUNK, (c + 1) * CHUNK)

@@ -21,6 +21,7 @@ PACK = 4
 K_PASS = P * PACK
 PASSES = K // K_PASS
 EPS = 1e-5
+HALF = S // 2
 CHUNK = 128
 CHUNKS = S // CHUNK
 
@@ -49,7 +50,7 @@ def tile_picked_inorm_relu_e_kernel(tc, xT, w1, w2_words, w2_scales, gamma, offs
         w2_codes = sb.tile([P, 2 * N], U8, name="w2_codes", align_bytes=64)
         w2_plane = sb.tile([P, N], U8, name="w2_plane", align_bytes=64)
         gam = sb.tile([P, PACK], F32, name="gam")
-        h = [ps.tile([P, S], F32, name=f"h{t}") for t in range(PACK)]
+        h = [[ps.tile([P, HALF], F32, name=f"h{t}{a}", tag=f"bank{2 * t + a}") for a in range(2)] for t in range(PACK)]
 
         def gather_x(g, j, lo, hi):
             nc.vector.tensor_copy(
@@ -78,15 +79,17 @@ def tile_picked_inorm_relu_e_kernel(tc, xT, w1, w2_words, w2_scales, gamma, offs
             )
 
         def product1(g, t):
-            nc.tensor.matmul_mx(
-                out=h[t][:],
-                lhsT=w_codes[g][t][:].bitcast(FP8X4),
-                lhsT_scale=w_scales[g][t][:],
-                rhs=x_codes[g][:].bitcast(FP8X4),
-                rhs_scale=x_scales[g][:],
-                start=(g == 0),
-                stop=(g == PASSES - 1),
-            )
+            for a in range(2):
+                cols = slice(a * HALF, (a + 1) * HALF)
+                nc.tensor.matmul_mx(
+                    out=h[t][a][:],
+                    lhsT=w_codes[g][t][:].bitcast(FP8X4),
+                    lhsT_scale=w_scales[g][t][:],
+                    rhs=x_codes[g][:, cols].bitcast(FP8X4),
+                    rhs_scale=x_scales[g][:, cols],
+                    start=(g == 0),
+                    stop=(g == PASSES - 1),
+                )
 
         nc.sync.dma_start(out=x_pair[0][:], in_=x_rows[0][:, 0:2, :])
         nc.sync.dma_start(offsets[:], offs)
@@ -147,31 +150,52 @@ def tile_picked_inorm_relu_e_kernel(tc, xT, w1, w2_words, w2_scales, gamma, offs
             product1(1, t)
 
         z_bf = sb.tile([P, S, PACK], BF16, name="z_bf", align_bytes=64)
-        post = []
+        stats = [sb.tile([P, 2, 6], F32, name=f"stats{t}") for t in range(PACK)]
+        post = [sb.tile([P, 2], F32, name=f"post{t}") for t in range(PACK)]
+
+        def half_stats(t, half):
+            nc.vector.bn_stats(out=stats[t][:, half, :], in_=h[t][half][:])
+
+        rstd_tiles = [sb.tile([P, 1], F32, name=f"rstd{t}") for t in range(PACK - 1)]
+        rstd = [tile[:] for tile in rstd_tiles] + [z_bf[:, 0, 0:2].bitcast(F32)]
+
+        def aggregate(t):
+            nc.vector.bn_aggr(out=moments[t][:, 1:3], in_=stats[t][:].rearrange("p a b -> p (a b)"))
+            nc.scalar.activation(out=rstd[t], in_=moments[t][:, 2:3], func=ACT.Abs_reciprocal_sqrt, bias=eps[t])
+
+        def scale_and_bias(t):
+            nc.vector.tensor_scalar(
+                out=post[t][:], in0=moments[t][:, 0:2], scalar1=rstd[t], scalar2=neg_gam[:, t : t + 1], op0=ALU.mult, op1=ALU.mult
+            )
+
+        def normalise(t, lo, hi):
+            a = lo // HALF
+            nc.scalar.activation(
+                out=z_flat[t // 2][:, t % 2, lo:hi],
+                in_=h[t][a][:, lo - a * HALF : hi - a * HALF],
+                func=ACT.Relu,
+                scale=post[t][:, 0:1],
+                bias=post[t][:, 1:2],
+            )
+
+        half_stats(0, 0)
         for t in range(PACK):
-            stats = sb.tile([P, 2, 6], F32, name=f"stats{t}")
-            for half in range(2):
-                nc.vector.bn_stats(out=stats[:, half, :], in_=h[t][:, half * (S // 2) : (half + 1) * (S // 2)])
-            nc.vector.bn_aggr(out=moments[t][:, 1:3], in_=stats[:].rearrange("p a b -> p (a b)"))
-            rstd = sb.tile([P, 1], F32, name=f"rstd{t}")
-            nc.scalar.activation(out=rstd[:], in_=moments[t][:, 2:3], func=ACT.Abs_reciprocal_sqrt, bias=eps[t])
-            ab = sb.tile([P, 2], F32, name=f"ab{t}")
-            nc.gpsimd.tensor_scalar(out=ab[:], in0=moments[t][:, 0:2], scalar1=rstd[:], scalar2=neg_gam[:, t : t + 1], op0=ALU.mult, op1=ALU.mult)
-            post.append(ab)
+            half_stats(t, 1)
+            if t + 1 < PACK:
+                half_stats(t + 1, 0)
+            aggregate(t)
             if t > 0:
-                s = t - 1
-                nc.scalar.activation(
-                    out=z_flat[s // 2][:, s % 2, :], in_=h[s][:], func=ACT.Relu, scale=post[s][:, 0:1], bias=post[s][:, 1:2]
-                )
+                scale_and_bias(t - 1)
+                normalise(t - 1, 0, HALF)
+                normalise(t - 1, HALF, S)
+        scale_and_bias(PACK - 1)
 
         nc.vector.tensor_copy(out=z_bf[:, :, 0:2], in_=z_flat[0][:].rearrange("p t s -> p s t"))
         last = PACK - 1
 
         def finish_z(c):
             cols = slice(c * CHUNK, (c + 1) * CHUNK)
-            nc.scalar.activation(
-                out=z_flat[1][:, 1, cols], in_=h[last][:, cols], func=ACT.Relu, scale=post[last][:, 0:1], bias=post[last][:, 1:2]
-            )
+            normalise(last, c * CHUNK, (c + 1) * CHUNK)
             copy = nc.scalar.copy if c == CHUNKS - 1 else nc.vector.tensor_copy
             copy(out=z_bf[:, cols, 2:4], in_=z_flat[1][:, :, cols].rearrange("p t s -> p s t"))
 
@@ -182,7 +206,7 @@ def tile_picked_inorm_relu_e_kernel(tc, xT, w1, w2_words, w2_scales, gamma, offs
             nc.vector.quantize_mx(
                 out=z_codes[:].bitcast(FP8X4), scales=z_scales[:], in_=z_bf[:, cols, :].rearrange("p s j -> p (s j)")
             )
-            acc = ps.tile([P, CHUNK], F32, name=f"acc{c}")
+            acc = ps.tile([P, CHUNK], F32, name=f"acc{c}", tag=f"bank{c}")
             nc.tensor.matmul_mx(
                 out=acc[:],
                 lhsT=w2_codes[:].bitcast(FP4X4),

@@ -21,9 +21,12 @@ PACK = 4
 K_PASS = P * PACK
 PASSES = K // K_PASS
 EPS = 1e-5
+STRIPE = 16
 HALF = S // 2
 CHUNK = 128
 CHUNKS = S // CHUNK
+DEAL_SPLIT = 96
+MX_ALIGN = 64
 
 
 def tile_picked_inorm_relu_e_kernel(tc, xT, w1, w2_words, w2_scales, gamma, offs, out):
@@ -32,7 +35,8 @@ def tile_picked_inorm_relu_e_kernel(tc, xT, w1, w2_words, w2_scales, gamma, offs
         sb = ctx.enter_context(tc.tile_pool(name="sb", bufs=1))
         ps = ctx.enter_context(tc.psum_pool(name="ps", bufs=1))
 
-        offsets = sb.tile([P, S // 16], U16, name="offsets")
+        offsets = sb.tile([P, S // STRIPE], U16, name="offsets")
+
         x_pair = [sb.tile([P, 2, T], F32, name=f"x_pair{u}") for u in range(2)]
         x_one = [sb.tile([P, T], F32, name=f"x_one{j}") for j in range(PACK)]
         x_raw = [[x_pair[j // 2][:, j % 2, :] for j in range(PACK)], [x_one[j][:] for j in range(PACK)]]
@@ -41,21 +45,22 @@ def tile_picked_inorm_relu_e_kernel(tc, xT, w1, w2_words, w2_scales, gamma, offs
         w_raw = [[w_whole[:, 2 * u : 2 * u + 2, :] for u in range(2)], [w_half[u][:] for u in range(2)]]
         x_rows = [xT[g * K_PASS : (g + 1) * K_PASS, :].rearrange("(p j) t -> p j t", j=PACK) for g in range(PASSES)]
         w_rows = [w1[g * K_PASS : (g + 1) * K_PASS, :].rearrange("(p j) c -> p j c", j=PACK) for g in range(PASSES)]
-        x_bf = [sb.tile([P, S, PACK], BF16, name=f"x_bf{g}", align_bytes=64) for g in range(PASSES)]
-        x_codes = [sb.tile([P, S], U32, name=f"x_codes{g}", align_bytes=64) for g in range(PASSES)]
-        x_scales = [sb.tile([P, S], U8, name=f"x_scales{g}", align_bytes=64) for g in range(PASSES)]
-        w_bf = [[sb.tile([P, 2, P, PACK], BF16, name=f"w_bf{g}{v}", align_bytes=64) for v in range(2)] for g in range(PASSES)]
-        w_codes = [[sb.tile([P, P], U32, name=f"w_codes{g}{t}", align_bytes=64) for t in range(PACK)] for g in range(PASSES)]
-        w_scales = [[sb.tile([P, P], U8, name=f"w_scales{g}{t}", align_bytes=64) for t in range(PACK)] for g in range(PASSES)]
-        w2_codes = sb.tile([P, 2 * N], U8, name="w2_codes", align_bytes=64)
-        w2_plane = sb.tile([P, N], U8, name="w2_plane", align_bytes=64)
+
+        x_bf = [sb.tile([P, S, PACK], BF16, name=f"x_bf{g}", align_bytes=MX_ALIGN) for g in range(PASSES)]
+        x_codes = [sb.tile([P, S], U32, name=f"x_codes{g}", align_bytes=MX_ALIGN) for g in range(PASSES)]
+        x_scales = [sb.tile([P, S], U8, name=f"x_scales{g}", align_bytes=MX_ALIGN) for g in range(PASSES)]
+        w_bf = [[sb.tile([P, 2, P, PACK], BF16, name=f"w_bf{g}{v}", align_bytes=MX_ALIGN) for v in range(2)] for g in range(PASSES)]
+        w_codes = [[sb.tile([P, P], U32, name=f"w_codes{g}{t}", align_bytes=MX_ALIGN) for t in range(PACK)] for g in range(PASSES)]
+        w_scales = [[sb.tile([P, P], U8, name=f"w_scales{g}{t}", align_bytes=MX_ALIGN) for t in range(PACK)] for g in range(PASSES)]
+        w2_codes = sb.tile([P, 2 * N], U8, name="w2_codes", align_bytes=MX_ALIGN)
+        w2_scale_rows = sb.tile([P, N], U8, name="w2_scale_rows", align_bytes=MX_ALIGN)
         gam = sb.tile([P, PACK], F32, name="gam")
         h = [[ps.tile([P, HALF], F32, name=f"h{t}{a}", tag=f"bank{2 * t + a}") for a in range(2)] for t in range(PACK)]
 
         def gather_x(g, j, lo, hi):
             nc.vector.tensor_copy(
                 out=x_bf[g][:, lo:hi, j],
-                in_=x_raw[g][j].indirect(offsets[:, lo // 16 : hi // 16]),
+                in_=x_raw[g][j].indirect(offsets[:, lo // STRIPE : hi // STRIPE]),
             )
 
         def quantize_x(g, lo, hi):
@@ -65,10 +70,10 @@ def tile_picked_inorm_relu_e_kernel(tc, xT, w1, w2_words, w2_scales, gamma, offs
                 in_=x_bf[g][:, lo:hi, :].rearrange("p s j -> p (s j)"),
             )
 
-        def deal_w(copy, g, u, v):
+        def deal_w(copy, g, u, v, lo=0, hi=P):
             copy(
-                out=w_bf[g][v][:, :, :, 2 * u : 2 * u + 2].rearrange("p t m j -> p m t j"),
-                in_=w_raw[g][u].rearrange("p j (m t) -> p m t j", t=PACK)[:, :, 2 * v : 2 * v + 2, :],
+                out=w_bf[g][v][:, :, lo:hi, 2 * u : 2 * u + 2].rearrange("p t m j -> p m t j"),
+                in_=w_raw[g][u].rearrange("p j (m t) -> p m t j", t=PACK)[:, lo:hi, 2 * v : 2 * v + 2, :],
             )
 
         def quantize_w(g, t):
@@ -100,29 +105,26 @@ def tile_picked_inorm_relu_e_kernel(tc, xT, w1, w2_words, w2_scales, gamma, offs
         for u in range(2):
             nc.sync.dma_start(out=w_half[u][:], in_=w_rows[1][:, 2 * u : 2 * u + 2, :])
 
-        nc.gpsimd.memset(w2_plane[:].bitcast(I32), 0)
+        nc.gpsimd.memset(w2_scale_rows[:].bitcast(I32), 0)
         nc.gpsimd.dma_start(out=gam[:], in_=gamma.rearrange("(p t) o -> p (t o)", t=PACK))
         nc.gpsimd.dma_start(out=w2_codes[:].bitcast(I32), in_=w2_words[0].bitcast(I32))
         for q in range(4):
             nc.gpsimd.dma_start(
-                out=w2_plane[32 * q : 32 * q + 4, :].bitcast(I32),
+                out=w2_scale_rows[32 * q : 32 * q + 4, :].bitcast(I32),
                 in_=w2_scales[0, 4 * q : 4 * q + 4, :].bitcast(I32),
             )
         neg_gam = sb.tile([P, PACK], F32, name="neg_gam")
         nc.gpsimd.tensor_scalar(out=neg_gam[:], in0=gam[:], scalar1=-1.0, scalar2=0.0, op0=ALU.mult, op1=ALU.add)
+
         moments = [sb.tile([P, 3], F32, name=f"moments{t}") for t in range(PACK)]
         for t in range(PACK):
             nc.vector.memset(moments[t][:, 0:1], -1.0)
+
         z_flat = [sb.tile([P, 2, S], BF16, name=f"z_flat{v}") for v in range(2)]
         eps_first = sb.tile([P, 1], F32, name="eps_first")
         eps = [eps_first[:]] + [z_flat[t // 2][:, t % 2, 0:2].bitcast(F32) for t in range(PACK - 1)]
         for t in range(PACK):
-            nc.vector.tensor_scalar(out=eps[t], in0=moments[0][:, 0:1], scalar1=-EPS, scalar2=None, op0=ALU.mult)
-
-        warm_in = sb.tile([P, 1], F32, name="warm_in")
-        warm_out = sb.tile([P, 1], F32, name="warm_out")
-        nc.vector.memset(warm_in[:], 1.0)
-        nc.scalar.activation(out=warm_out[:], in_=warm_in[:], func=ACT.Abs_reciprocal_sqrt, bias=EPS)
+            nc.scalar.activation(out=eps[t], in_=moments[0][:, 0:1], func=ACT.Abs_reciprocal_sqrt, scale=EPS**-2)
 
         for j in range(PACK):
             gather_x(0, j, 0, S)
@@ -137,27 +139,28 @@ def tile_picked_inorm_relu_e_kernel(tc, xT, w1, w2_words, w2_scales, gamma, offs
 
         gather_x(1, 1, 0, S)
         gather_x(1, 2, 0, S)
-        gather_x(1, 3, 0, S // 2)
-        gather_x(1, 3, S // 2, S)
-        quantize_x(1, 0, S // 2)
-        quantize_x(1, S // 2, S)
+        gather_x(1, 3, 0, HALF)
+        gather_x(1, 3, HALF, S)
+        quantize_x(1, 0, HALF)
+        quantize_x(1, HALF, S)
         deal_w(nc.scalar.copy, 1, 0, 0)
         deal_w(nc.scalar.copy, 1, 0, 1)
         deal_w(nc.vector.tensor_copy, 1, 1, 0)
-        deal_w(nc.scalar.copy, 1, 1, 1)
+        deal_w(nc.vector.tensor_copy, 1, 1, 1, 0, DEAL_SPLIT)
+        deal_w(nc.scalar.copy, 1, 1, 1, DEAL_SPLIT, P)
         for t in range(PACK):
             quantize_w(1, t)
             product1(1, t)
 
-        z_bf = sb.tile([P, S, PACK], BF16, name="z_bf", align_bytes=64)
+        z_bf = sb.tile([P, S, PACK], BF16, name="z_bf", align_bytes=MX_ALIGN)
         stats = [sb.tile([P, 2, 6], F32, name=f"stats{t}") for t in range(PACK)]
-        post = [sb.tile([P, 2], F32, name=f"post{t}") for t in range(PACK)]
+        affine = [sb.tile([P, 2], F32, name=f"affine{t}") for t in range(PACK)]
+        last = PACK - 1
+        rstd_tiles = [sb.tile([P, 1], F32, name=f"rstd{t}") for t in range(last)]
+        rstd = [tile[:] for tile in rstd_tiles] + [z_bf[:, HALF, 0:2].bitcast(F32)]
 
-        def half_stats(t, half):
-            nc.vector.bn_stats(out=stats[t][:, half, :], in_=h[t][half][:])
-
-        rstd_tiles = [sb.tile([P, 1], F32, name=f"rstd{t}") for t in range(PACK - 1)]
-        rstd = [tile[:] for tile in rstd_tiles] + [z_bf[:, 0, 0:2].bitcast(F32)]
+        def half_stats(t, a):
+            nc.vector.bn_stats(out=stats[t][:, a, :], in_=h[t][a][:])
 
         def aggregate(t):
             nc.vector.bn_aggr(out=moments[t][:, 1:3], in_=stats[t][:].rearrange("p a b -> p (a b)"))
@@ -165,7 +168,7 @@ def tile_picked_inorm_relu_e_kernel(tc, xT, w1, w2_words, w2_scales, gamma, offs
 
         def scale_and_bias(t):
             nc.vector.tensor_scalar(
-                out=post[t][:], in0=moments[t][:, 0:2], scalar1=rstd[t], scalar2=neg_gam[:, t : t + 1], op0=ALU.mult, op1=ALU.mult
+                out=affine[t][:], in0=moments[t][:, 0:2], scalar1=rstd[t], scalar2=neg_gam[:, t : t + 1], op0=ALU.mult, op1=ALU.mult
             )
 
         def normalise(t, lo, hi):
@@ -174,24 +177,25 @@ def tile_picked_inorm_relu_e_kernel(tc, xT, w1, w2_words, w2_scales, gamma, offs
                 out=z_flat[t // 2][:, t % 2, lo:hi],
                 in_=h[t][a][:, lo - a * HALF : hi - a * HALF],
                 func=ACT.Relu,
-                scale=post[t][:, 0:1],
-                bias=post[t][:, 1:2],
+                scale=affine[t][:, 0:1],
+                bias=affine[t][:, 1:2],
             )
 
         half_stats(0, 0)
         for t in range(PACK):
             half_stats(t, 1)
-            if t + 1 < PACK:
+            if t < last:
                 half_stats(t + 1, 0)
             aggregate(t)
             if t > 0:
                 scale_and_bias(t - 1)
                 normalise(t - 1, 0, HALF)
                 normalise(t - 1, HALF, S)
-        scale_and_bias(PACK - 1)
+        scale_and_bias(last)
 
-        nc.vector.tensor_copy(out=z_bf[:, :, 0:2], in_=z_flat[0][:].rearrange("p t s -> p s t"))
-        last = PACK - 1
+        for a in range(2):
+            cols = slice(a * HALF, (a + 1) * HALF)
+            nc.vector.tensor_copy(out=z_bf[:, cols, 0:2], in_=z_flat[0][:, :, cols].rearrange("p t s -> p s t"))
 
         def finish_z(c):
             cols = slice(c * CHUNK, (c + 1) * CHUNK)
@@ -201,8 +205,8 @@ def tile_picked_inorm_relu_e_kernel(tc, xT, w1, w2_words, w2_scales, gamma, offs
 
         def product2(c):
             cols = slice(c * CHUNK, (c + 1) * CHUNK)
-            z_codes = sb.tile([P, CHUNK], U32, name=f"z_codes{c}", align_bytes=64)
-            z_scales = sb.tile([P, CHUNK], U8, name=f"z_scales{c}", align_bytes=64)
+            z_codes = sb.tile([P, CHUNK], U32, name=f"z_codes{c}", align_bytes=MX_ALIGN)
+            z_scales = sb.tile([P, CHUNK], U8, name=f"z_scales{c}", align_bytes=MX_ALIGN)
             nc.vector.quantize_mx(
                 out=z_codes[:].bitcast(FP8X4), scales=z_scales[:], in_=z_bf[:, cols, :].rearrange("p s j -> p (s j)")
             )
@@ -210,7 +214,7 @@ def tile_picked_inorm_relu_e_kernel(tc, xT, w1, w2_words, w2_scales, gamma, offs
             nc.tensor.matmul_mx(
                 out=acc[:],
                 lhsT=w2_codes[:].bitcast(FP4X4),
-                lhsT_scale=w2_plane[:],
+                lhsT_scale=w2_scale_rows[:],
                 rhs=z_codes[:].bitcast(FP8X4),
                 rhs_scale=z_scales[:],
                 start=True,
@@ -219,10 +223,9 @@ def tile_picked_inorm_relu_e_kernel(tc, xT, w1, w2_words, w2_scales, gamma, offs
             return acc
 
         def store(c, acc):
-            cols = slice(c * CHUNK, (c + 1) * CHUNK)
             result = sb.tile([P, CHUNK], F32, name=f"result{c}")
             nc.scalar.copy(out=result[:], in_=acc[:])
-            nc.sync.dma_start(out=out[:, cols], in_=result[:])
+            nc.sync.dma_start(out=out[:, c * CHUNK : (c + 1) * CHUNK], in_=result[:])
 
         accs = []
         finish_z(0)

from contextlib import ExitStack

import concourse.mybir as mybir

K, T, S, H, N = 1024, 2048, 512, 512, 128
FLOPS = 2 * K * H * S + 2 * H * N * S

F32 = mybir.dt.float32
BF16 = mybir.dt.bfloat16
U32 = mybir.dt.uint32
I32 = mybir.dt.int32
U16 = mybir.dt.uint16
U8 = mybir.dt.uint8
FP8X4 = mybir.dt.float8_e4m3fn_x4
FP4X4 = mybir.dt.float4_e2m1fn_x4
ACT = mybir.ActivationFunctionType
ALU = mybir.AluOpType

P = 128
PACK = 4
K_PASS = P * PACK
PASSES = K // K_PASS
EPS = 1e-5
STRIPE = 16
HALF = S // 2
CHUNK = 128
CHUNKS = S // CHUNK
DEAL_SPLIT = 96
MX_ALIGN = 64


def tile_picked_inorm_relu_e_kernel(tc, xT, w1, w2_words, w2_scales, gamma, offs, out):
    nc = tc.nc
    with ExitStack() as ctx:
        sb = ctx.enter_context(tc.tile_pool(name="sb", bufs=1))
        ps = ctx.enter_context(tc.psum_pool(name="ps", bufs=1))

        offsets = sb.tile([P, S // STRIPE], U16, name="offsets")

        x_pair = [sb.tile([P, 2, T], F32, name=f"x_pair{u}") for u in range(2)]
        x_one = [sb.tile([P, T], F32, name=f"x_one{j}") for j in range(PACK)]
        x_raw = [[x_pair[j // 2][:, j % 2, :] for j in range(PACK)], [x_one[j][:] for j in range(PACK)]]
        w_whole = sb.tile([P, PACK, H], F32, name="w_whole")
        w_half = [sb.tile([P, 2, H], F32, name=f"w_half{u}") for u in range(2)]
        w_raw = [[w_whole[:, 2 * u : 2 * u + 2, :] for u in range(2)], [w_half[u][:] for u in range(2)]]
        x_rows = [xT[g * K_PASS : (g + 1) * K_PASS, :].rearrange("(p j) t -> p j t", j=PACK) for g in range(PASSES)]
        w_rows = [w1[g * K_PASS : (g + 1) * K_PASS, :].rearrange("(p j) c -> p j c", j=PACK) for g in range(PASSES)]

        x_bf = [sb.tile([P, S, PACK], BF16, name=f"x_bf{g}", align_bytes=MX_ALIGN) for g in range(PASSES)]
        x_codes = [sb.tile([P, S], U32, name=f"x_codes{g}", align_bytes=MX_ALIGN) for g in range(PASSES)]
        x_scales = [sb.tile([P, S], U8, name=f"x_scales{g}", align_bytes=MX_ALIGN) for g in range(PASSES)]
        w_bf = [[sb.tile([P, 2, P, PACK], BF16, name=f"w_bf{g}{v}", align_bytes=MX_ALIGN) for v in range(2)] for g in range(PASSES)]
        w_codes = [[sb.tile([P, P], U32, name=f"w_codes{g}{t}", align_bytes=MX_ALIGN) for t in range(PACK)] for g in range(PASSES)]
        w_scales = [[sb.tile([P, P], U8, name=f"w_scales{g}{t}", align_bytes=MX_ALIGN) for t in range(PACK)] for g in range(PASSES)]
        w2_codes = sb.tile([P, 2 * N], U8, name="w2_codes", align_bytes=MX_ALIGN)
        w2_scale_rows = sb.tile([P, N], U8, name="w2_scale_rows", align_bytes=MX_ALIGN)
        gam = sb.tile([P, PACK], F32, name="gam")
        h = [[ps.tile([P, HALF], F32, name=f"h{t}{a}", tag=f"bank{2 * t + a}") for a in range(2)] for t in range(PACK)]

        def gather_x(g, j, lo, hi):
            nc.vector.tensor_copy(
                out=x_bf[g][:, lo:hi, j],
                in_=x_raw[g][j].indirect(offsets[:, lo // STRIPE : hi // STRIPE]),
            )

        def quantize_x(g, lo, hi):
            nc.vector.quantize_mx(
                out=x_codes[g][:, lo:hi].bitcast(FP8X4),
                scales=x_scales[g][:, lo:hi],
                in_=x_bf[g][:, lo:hi, :].rearrange("p s j -> p (s j)"),
            )

        def deal_w(copy, g, u, v, lo=0, hi=P):
            copy(
                out=w_bf[g][v][:, :, lo:hi, 2 * u : 2 * u + 2].rearrange("p t m j -> p m t j"),
                in_=w_raw[g][u].rearrange("p j (m t) -> p m t j", t=PACK)[:, lo:hi, 2 * v : 2 * v + 2, :],
            )

        def quantize_w(g, t):
            nc.vector.quantize_mx(
                out=w_codes[g][t][:].bitcast(FP8X4),
                scales=w_scales[g][t][:],
                in_=w_bf[g][t // 2][:, t % 2, :, :].rearrange("p m j -> p (m j)"),
            )

        def product1(g, t):
            for a in range(2):
                cols = slice(a * HALF, (a + 1) * HALF)
                nc.tensor.matmul_mx(
                    out=h[t][a][:],
                    lhsT=w_codes[g][t][:].bitcast(FP8X4),
                    lhsT_scale=w_scales[g][t][:],
                    rhs=x_codes[g][:, cols].bitcast(FP8X4),
                    rhs_scale=x_scales[g][:, cols],
                    start=(g == 0),
                    stop=(g == PASSES - 1),
                )

        nc.sync.dma_start(out=x_pair[0][:], in_=x_rows[0][:, 0:2, :])
        nc.sync.dma_start(offsets[:], offs)
        nc.sync.dma_start(out=x_pair[1][:], in_=x_rows[0][:, 2:4, :])
        nc.sync.dma_start(out=w_whole[:], in_=w_rows[0])
        for j in range(PACK):
            nc.sync.dma_start(out=x_one[j][:], in_=x_rows[1][:, j, :])
        for u in range(2):
            nc.sync.dma_start(out=w_half[u][:], in_=w_rows[1][:, 2 * u : 2 * u + 2, :])

        nc.gpsimd.memset(w2_scale_rows[:].bitcast(I32), 0)
        nc.gpsimd.dma_start(out=gam[:], in_=gamma.rearrange("(p t) o -> p (t o)", t=PACK))
        nc.gpsimd.dma_start(out=w2_codes[:].bitcast(I32), in_=w2_words[0].bitcast(I32))
        for q in range(4):
            nc.gpsimd.dma_start(
                out=w2_scale_rows[32 * q : 32 * q + 4, :].bitcast(I32),
                in_=w2_scales[0, 4 * q : 4 * q + 4, :].bitcast(I32),
            )
        neg_gam = sb.tile([P, PACK], F32, name="neg_gam")
        nc.gpsimd.tensor_scalar(out=neg_gam[:], in0=gam[:], scalar1=-1.0, scalar2=0.0, op0=ALU.mult, op1=ALU.add)

        moments = [sb.tile([P, 3], F32, name=f"moments{t}") for t in range(PACK)]
        for t in range(PACK):
            nc.vector.memset(moments[t][:, 0:1], -1.0)

        z_flat = [sb.tile([P, 2, S], BF16, name=f"z_flat{v}") for v in range(2)]
        eps_first = sb.tile([P, 1], F32, name="eps_first")
        eps = [eps_first[:]] + [z_flat[t // 2][:, t % 2, 0:2].bitcast(F32) for t in range(PACK - 1)]
        for t in range(PACK):
            nc.scalar.activation(out=eps[t], in_=moments[0][:, 0:1], func=ACT.Abs_reciprocal_sqrt, scale=EPS**-2)

        for j in range(PACK):
            gather_x(0, j, 0, S)
        quantize_x(0, 0, S)
        for u in range(2):
            for v in range(2):
                deal_w(nc.scalar.copy, 0, u, v)
        gather_x(1, 0, 0, S)
        for t in range(PACK):
            quantize_w(0, t)
            product1(0, t)

        gather_x(1, 1, 0, S)
        gather_x(1, 2, 0, S)
        gather_x(1, 3, 0, HALF)
        gather_x(1, 3, HALF, S)
        quantize_x(1, 0, HALF)
        quantize_x(1, HALF, S)
        deal_w(nc.scalar.copy, 1, 0, 0)
        deal_w(nc.scalar.copy, 1, 0, 1)
        deal_w(nc.vector.tensor_copy, 1, 1, 0)
        deal_w(nc.vector.tensor_copy, 1, 1, 1, 0, DEAL_SPLIT)
        deal_w(nc.scalar.copy, 1, 1, 1, DEAL_SPLIT, P)
        for t in range(PACK):
            quantize_w(1, t)
            product1(1, t)

        z_bf = sb.tile([P, S, PACK], BF16, name="z_bf", align_bytes=MX_ALIGN)
        stats = [sb.tile([P, 2, 6], F32, name=f"stats{t}") for t in range(PACK)]
        affine = [sb.tile([P, 2], F32, name=f"affine{t}") for t in range(PACK)]
        last = PACK - 1
        rstd_tiles = [sb.tile([P, 1], F32, name=f"rstd{t}") for t in range(last)]
        rstd = [tile[:] for tile in rstd_tiles] + [z_bf[:, HALF, 0:2].bitcast(F32)]

        def half_stats(t, a):
            nc.vector.bn_stats(out=stats[t][:, a, :], in_=h[t][a][:])

        def aggregate(t):
            nc.vector.bn_aggr(out=moments[t][:, 1:3], in_=stats[t][:].rearrange("p a b -> p (a b)"))
            nc.scalar.activation(out=rstd[t], in_=moments[t][:, 2:3], func=ACT.Abs_reciprocal_sqrt, bias=eps[t])

        def scale_and_bias(t):
            nc.vector.tensor_scalar(
                out=affine[t][:], in0=moments[t][:, 0:2], scalar1=rstd[t], scalar2=neg_gam[:, t : t + 1], op0=ALU.mult, op1=ALU.mult
            )

        def normalise(t, lo, hi):
            a = lo // HALF
            nc.scalar.activation(
                out=z_flat[t // 2][:, t % 2, lo:hi],
                in_=h[t][a][:, lo - a * HALF : hi - a * HALF],
                func=ACT.Relu,
                scale=affine[t][:, 0:1],
                bias=affine[t][:, 1:2],
            )

        half_stats(0, 0)
        for t in range(PACK):
            half_stats(t, 1)
            if t < last:
                half_stats(t + 1, 0)
            aggregate(t)
            if t > 0:
                scale_and_bias(t - 1)
                normalise(t - 1, 0, HALF)
                normalise(t - 1, HALF, S)
        scale_and_bias(last)

        for a in range(2):
            cols = slice(a * HALF, (a + 1) * HALF)
            nc.vector.tensor_copy(out=z_bf[:, cols, 0:2], in_=z_flat[0][:, :, cols].rearrange("p t s -> p s t"))

        def finish_z(c):
            cols = slice(c * CHUNK, (c + 1) * CHUNK)
            normalise(last, c * CHUNK, (c + 1) * CHUNK)
            copy = nc.scalar.copy if c == CHUNKS - 1 else nc.vector.tensor_copy
            copy(out=z_bf[:, cols, 2:4], in_=z_flat[1][:, :, cols].rearrange("p t s -> p s t"))

        def product2(c):
            cols = slice(c * CHUNK, (c + 1) * CHUNK)
            z_codes = sb.tile([P, CHUNK], U32, name=f"z_codes{c}", align_bytes=MX_ALIGN)
            z_scales = sb.tile([P, CHUNK], U8, name=f"z_scales{c}", align_bytes=MX_ALIGN)
            nc.vector.quantize_mx(
                out=z_codes[:].bitcast(FP8X4), scales=z_scales[:], in_=z_bf[:, cols, :].rearrange("p s j -> p (s j)")
            )
            acc = ps.tile([P, CHUNK], F32, name=f"acc{c}", tag=f"bank{c}")
            nc.tensor.matmul_mx(
                out=acc[:],
                lhsT=w2_codes[:].bitcast(FP4X4),
                lhsT_scale=w2_scale_rows[:],
                rhs=z_codes[:].bitcast(FP8X4),
                rhs_scale=z_scales[:],
                start=True,
                stop=True,
            )
            return acc

        def store(c, acc):
            result = sb.tile([P, CHUNK], F32, name=f"result{c}")
            nc.scalar.copy(out=result[:], in_=acc[:])
            nc.sync.dma_start(out=out[:, c * CHUNK : (c + 1) * CHUNK], in_=result[:])

        accs = []
        finish_z(0)
        for c in range(CHUNKS):
            if c + 1 < CHUNKS:
                finish_z(c + 1)
            accs.append(product2(c))
        for c in range(CHUNKS):
            store(c, accs[c])
